import numpy as np
import ml_dtypes


def mxq(x, axis, fmt="e4m3"):
    dtype, down = {"e4m3": (ml_dtypes.float8_e4m3fn, 7), "e5m2": (ml_dtypes.float8_e5m2, 14)}[fmt]
    v = np.moveaxis(np.asarray(x, np.float32).astype(ml_dtypes.bfloat16).astype(np.float64), axis, -1)
    blocks = v.reshape(v.shape[:-1] + (-1, 32))
    amax = np.abs(blocks).max(-1, keepdims=True)
    byte = np.maximum(np.where(amax > 0, np.frexp(amax)[1] - 1 + 127, 0) - down, 1)
    scale = np.exp2(byte - 127.0)
    codes = (blocks / scale).astype(np.float32).astype(dtype).astype(np.float64)
    return np.moveaxis((codes * scale).reshape(v.shape), -1, axis)


WIDE = False


def mx_kscale(k):
    if not WIDE:
        return np.ones(k)
    levels = np.array([10, -10, 5, -5, 0])
    if k % 512:
        return np.exp2(np.random.permutation(np.resize(levels, k // 32))).repeat(32)
    a = np.empty((k // 512, 16))
    for p in range(k // 512):
        a[p, :8] = np.random.permutation(np.resize(levels, 8))
        for g in range(8):
            far = levels[np.abs(levels - a[p, g]) >= 10]
            a[p, g + 8] = far[np.random.randint(len(far))]
    return np.exp2(a.ravel()).repeat(32)


def f64(x):
    return np.asarray(x).astype(np.float64)


def striped(idx):
    return np.tile(idx.reshape(-1, 16).T, (8, 1)).astype(np.uint16)


def unstriped(offs):
    return offs[:16].T.reshape(-1).astype(np.int64)


def pack_weight(w):
    k, n = w.shape
    w = f64(np.asarray(w, np.float32).astype(ml_dtypes.bfloat16)).reshape(k // 32, 32, n)
    amax = np.abs(w).max(1)
    byte = np.clip(np.where(amax > 0, np.frexp(amax)[1] - 1 + 127 - 7, 1), 1, 254)
    scaled = (w * np.exp2(127.0 - byte)[:, None, :]).reshape(k, n).astype(np.float32)
    words = np.ascontiguousarray(scaled.reshape(k // 512, 128, 4, n).transpose(0, 1, 3, 2)).astype(ml_dtypes.float8_e4m3fn).view(np.uint8)
    return words, np.ascontiguousarray(byte.astype(np.uint8).reshape(k // 512, 16, n))


def unpack_weight(words, scales):
    g, p, n, _ = words.shape
    vals = np.ascontiguousarray(words).view(ml_dtypes.float8_e4m3fn).astype(np.float64) * np.repeat(np.exp2(scales.astype(np.float64) - 127.0), 8, axis=1)[..., None]
    return vals.transpose(0, 1, 3, 2).reshape(g * 512, n)


K, T, S, D, N, U = 512, 2048, 512, 4, 128, 1024


def setup_inputs():
    n = np.random.standard_normal
    s = mx_kscale(K)[:, None]
    packed_xT = pack_weight(n((K, T)) * s)
    return {
        "x_words": packed_xT[0],
        "x_scales": packed_xT[1],
        "w1": (n((K, N)) / np.sqrt(K) / s).astype(np.float32),
        "avg": (np.random.uniform(0.3, 2.0, (N, U))).astype(np.float32),
        "offs": striped(np.random.permutation(T)[:S]),
        "usr": striped(np.random.permutation(U)[:S]),
    }


def reference(x_words, x_scales, w1, avg, offs, usr):
    ag = f64(avg)[:, unstriped(usr)]
    xq = unpack_weight(x_words, x_scales)[:, unstriped(offs)]
    y = mxq(f64(w1), 0, "e4m3").T @ xq
    rate = np.log(np.exp(y) + 1.0)
    met = rate / ag
    m3 = 3.0 * met
    top = m3.reshape(len(m3), -1, D).max(axis=2)
    ex = np.exp(m3 - np.repeat(top, D, axis=1))
    total = ex.reshape(len(ex), -1, D).sum(axis=2)
    share = ex / np.repeat(total, D, axis=1)
    na = 0.8 * ag + 0.2 * (share * rate)
    out = f64(avg).copy()
    out[:, unstriped(usr)] = na
    return out

@@ -1,0 +1,177 @@
+from contextlib import ExitStack
+
+import concourse.mybir as mybir
+
+F32 = mybir.dt.float32
+BF16 = mybir.dt.bfloat16
+I32 = mybir.dt.int32
+U32 = mybir.dt.uint32
+U16 = mybir.dt.uint16
+U8 = mybir.dt.uint8
+FP8X4 = mybir.dt.float8_e4m3fn_x4
+ALU = mybir.AluOpType
+ACT = mybir.ActivationFunctionType
+AXIS_X = mybir.AxisListType.X
+
+P = 128
+K, T, S, D, N, U = 512, 2048, 512, 4, 128, 1024
+HALVES = 2
+HALF = S // HALVES
+GROUPS = HALF // D
+AVG_WINDOW = 2 * U
+TINY = 2.0 ** -60
+
+FLOPS = 2 * K * N * S
+
+
+def tile_picked_ypf_put_p_kernel(tc, x_words, x_scales, w1, avg, offs, usr, out):
+    nc = tc.nc
+    with ExitStack() as ctx:
+        sb = ctx.enter_context(tc.tile_pool(name="sb", bufs=1))
+        ps = ctx.enter_context(tc.psum_pool(name="ps", bufs=1))
+
+        offs_sb = sb.tile([P, S // 16], U16, name="offs_sb")
+        usr_sb = sb.tile([P, S // 16], U16, name="usr_sb")
+        xw = sb.tile([P, T], I32, name="xw", align_bytes=64)
+        xs = sb.tile([P, T], U8, name="xs", align_bytes=64)
+        w_raw = sb.tile([P, 4, N], F32, name="w_raw")
+        window = sb.tile([P, AVG_WINDOW], F32, name="window", align_bytes=64)
+        tiny = sb.tile([P, 1], F32, name="tiny")
+
+        nc.vector.memset(xs[:].bitcast(I32), 0)
+        nc.gpsimd.memset(window[:, U:], 0.0)
+        nc.gpsimd.memset(tiny[:], TINY)
+
+        nc.sync.dma_start(offs_sb[:], offs)
+        nc.sync.dma_start(w_raw[:], w1.rearrange("(p j) n -> p j n", j=4))
+        for q in range(4):
+            nc.sync.dma_start(xs[32 * q : 32 * q + 4, :].bitcast(I32), x_scales[0, 4 * q : 4 * q + 4, :].bitcast(I32))
+        nc.sync.dma_start(xw[:], x_words[0].rearrange("p c r -> p (c r)").bitcast(I32))
+        nc.sync.dma_start(usr_sb[:], usr)
+        nc.sync.dma_start(window[:, :U], avg)
+
+        w_bf = sb.tile([P, N, 4], BF16, name="w_bf", align_bytes=64)
+        w_codes = sb.tile([P, N], U32, name="w_codes", align_bytes=64)
+        w_scales = sb.tile([P, N], U8, name="w_scales", align_bytes=64)
+        nc.scalar.copy(w_bf[:], w_raw[:].rearrange("p j n -> p n j"))
+        gs = sb.tile([P, S], U8, name="gs", align_bytes=64)
+        nc.vector.tensor_copy(gs[:], xs[:].indirect(offs_sb[:]))
+        nc.vector.quantize_mx(out=w_codes[:].bitcast(FP8X4), scales=w_scales[:], in_=w_bf[:].rearrange("p n j -> p (n j)"))
+
+        cols = [slice(h * HALF, (h + 1) * HALF) for h in range(HALVES)]
+        lcols = [slice(h * HALF // 16, (h + 1) * HALF // 16) for h in range(HALVES)]
+        sig = sb.tile([P, S], F32, name="sig")
+        y = []
+        for h in range(HALVES):
+            gw = sb.tile([P, HALF], U32, name="gw%d" % h, align_bytes=64)
+            nc.vector.tensor_copy(gw[:], xw[:].bitcast(U32).indirect(offs_sb[:, lcols[h]]))
+            yh = ps.tile([P, HALF], F32, name="y%d" % h)
+            nc.tensor.matmul_mx(out=yh[:], lhsT=w_codes[:].bitcast(FP8X4), lhsT_scale=w_scales[:],
+                                rhs=gw[:].bitcast(FP8X4), rhs_scale=gs[:, cols[h]], start=True, stop=True)
+            nc.scalar.activation(sig[:, cols[h]], yh[:], ACT.Sigmoid, scale=-1.0)
+            y.append(yh)
+        lns = sb.tile([P, S], F32, name="lns")
+        nc.scalar.activation(lns[:], sig[:], ACT.Ln, bias=tiny[:])
+
+        kept = sb.tile([P, S], F32, name="kept")
+        nc.vector.tensor_scalar(kept[:], window[:].indirect(usr_sb[:]), 0.8, 0.0, ALU.mult, ALU.add)
+
+        def half_tiles(name, width):
+            return [sb.tile([P, width], F32, name="%s%d" % (name, h)) for h in range(HALVES)]
+
+        pair = half_tiles("pair", GROUPS * 2)
+        prod = half_tiles("prod", GROUPS)
+        rprod = half_tiles("rprod", GROUPS)
+        rpair = half_tiles("rpair", GROUPS * 2)
+        rkept = half_tiles("rkept", HALF)
+        k4 = [kept[:, cols[h]].rearrange("p (v a e) -> p v a e", a=2, e=2) for h in range(HALVES)]
+        H = range(HALVES)
+        rate = half_tiles("rate", HALF)
+        met = half_tiles("met", HALF)
+        top = half_tiles("top", GROUPS)
+        diff = half_tiles("diff", HALF)
+        ex = half_tiles("ex", HALF)
+        total = half_tiles("total", GROUPS)
+        rtotal = half_tiles("rtotal", GROUPS)
+        exrate = half_tiles("exrate", HALF)
+        gain = sb.tile([P, S], F32, name="gain")
+
+        def grouped(t):
+            return t.rearrange("p (v d) -> p v d", d=D)
+
+        def paired(t):
+            return t.rearrange("p (v e) -> p v e", e=2)
+
+        def spread(t):
+            return t.unsqueeze(2).to_broadcast([P, GROUPS, D])
+
+        def s_pair(h):
+            nc.vector.tensor_tensor(paired(pair[h][:]), k4[h][:, :, 0, :], k4[h][:, :, 1, :], ALU.mult)
+
+        def s_prod(h):
+            nc.vector.tensor_tensor(prod[h][:], pair[h][:, 0::2], pair[h][:, 1::2], ALU.mult)
+
+        def s_rprod(h):
+            nc.vector.reciprocal(rprod[h][:], prod[h][:])
+
+        def s_rpair(h):
+            nc.vector.tensor_tensor(paired(rpair[h][:]), paired(pair[h][:])[:, :, ::-1],
+                                    rprod[h][:].unsqueeze(2).to_broadcast([P, GROUPS, 2]), ALU.mult)
+
+        def s_rkept(h):
+            nc.vector.tensor_tensor(rkept[h][:].rearrange("p (v a e) -> p v a e", a=2, e=2), k4[h][:, :, ::-1, :],
+                                    paired(rpair[h][:]).unsqueeze(2).to_broadcast([P, GROUPS, 2, 2]), ALU.mult)
+
+        def s_rate(h):
+            nc.vector.scalar_tensor_tensor(rate[h][:], lns[:, cols[h]], -1.0, y[h][:], ALU.mult, ALU.max)
+
+        def s_met(h):
+            nc.vector.tensor_tensor(met[h][:], rate[h][:], rkept[h][:], ALU.mult)
+
+        def s_top(h):
+            nc.vector.tensor_reduce(top[h][:], grouped(met[h][:]), AXIS_X, ALU.max)
+
+        def s_ex(h):
+            nc.vector.tensor_tensor(grouped(diff[h][:]), grouped(met[h][:]), spread(top[h][:]), ALU.subtract)
+            nc.scalar.activation(ex[h][:], diff[h][:], ACT.Exp, scale=3.0 * 0.8)
+
+        def s_total(h):
+            nc.vector.tensor_reduce(total[h][:], grouped(ex[h][:]), AXIS_X, ALU.add)
+
+        def s_exrate(h):
+            nc.vector.tensor_tensor(exrate[h][:], ex[h][:], rate[h][:], ALU.mult)
+
+        def s_rtotal(h):
+            nc.vector.reciprocal(rtotal[h][:], total[h][:])
+
+        def s_gain(h):
+            nc.vector.scalar_tensor_tensor(grouped(gain[:, cols[h]]), grouped(exrate[h][:]), 0.2, spread(rtotal[h][:]), ALU.mult, ALU.mult)
+
+        s_pair(0)
+        s_pair(1)
+        s_prod(0)
+        s_prod(1)
+        s_rprod(0)
+        s_rprod(1)
+        s_rpair(0)
+        s_rpair(1)
+        s_rkept(0)
+        s_rate(0)
+        s_rkept(1)
+        s_met(0)
+        s_rate(1)
+        s_top(0)
+        s_met(1)
+        s_ex(0)
+        s_top(1)
+        s_ex(1)
+        s_total(0)
+        s_exrate(0)
+        s_rtotal(0)
+        s_total(1)
+        s_exrate(1)
+        s_rtotal(1)
+        s_gain(0)
+        s_gain(1)
+        nc.vector.tensor_tensor(window[:].indirect(usr_sb[:]), gain[:], kept[:], ALU.add)
+        nc.sync.dma_start(out, window[:, :U])

@@ -44,8 +44,8 @@ def tile_picked_ypf_put_p_kernel(tc, x_words, x_scales, w1, avg, offs, usr, out)
 
         nc.sync.dma_start(offs_sb[:], offs)
         nc.sync.dma_start(w_raw[:], w1.rearrange("(p j) n -> p j n", j=4))
-        for q in range(4):
-            nc.sync.dma_start(xs[32 * q : 32 * q + 4, :].bitcast(I32), x_scales[0, 4 * q : 4 * q + 4, :].bitcast(I32))
+        for r in range(4):
+            nc.sync.dma_start(xs[r:P:32, :].bitcast(I32), x_scales[0, r:16:4, :].bitcast(I32))
         nc.sync.dma_start(xw[:], x_words[0].rearrange("p c r -> p (c r)").bitcast(I32))
         nc.sync.dma_start(usr_sb[:], usr)
         nc.sync.dma_start(window[:, :U], avg)
@@ -70,8 +70,10 @@ def tile_picked_ypf_put_p_kernel(tc, x_words, x_scales, w1, avg, offs, usr, out)
                                 rhs=gw[:].bitcast(FP8X4), rhs_scale=gs[:, cols[h]], start=True, stop=True)
             nc.scalar.activation(sig[:, cols[h]], yh[:], ACT.Sigmoid, scale=-1.0)
             y.append(yh)
-        lns = sb.tile([P, S], F32, name="lns")
-        nc.scalar.activation(lns[:], sig[:], ACT.Ln, bias=tiny[:])
+        ln_lead = sb.tile([P, HALF], F32, name="ln_lead")
+        lns = [sig[:, cols[1]], ln_lead[:]]
+        nc.scalar.activation(lns[1], sig[:, cols[1]], ACT.Ln, bias=tiny[:])
+        nc.scalar.activation(lns[0], sig[:, cols[0]], ACT.Ln, bias=tiny[:])
 
         kept = sb.tile([P, S], F32, name="kept")
         nc.vector.tensor_scalar(kept[:], window[:].indirect(usr_sb[:]), 0.8, 0.0, ALU.mult, ALU.add)
@@ -79,14 +81,15 @@ def tile_picked_ypf_put_p_kernel(tc, x_words, x_scales, w1, avg, offs, usr, out)
         def half_tiles(name, width):
             return [sb.tile([P, width], F32, name="%s%d" % (name, h)) for h in range(HALVES)]
 
-        pair = half_tiles("pair", GROUPS * 2)
+        rate = half_tiles("rate", HALF)
+        spare = half_tiles("spare", GROUPS * 2)
+        pair = [spare[0][:], rate[1][:, : GROUPS * 2]]
         prod = half_tiles("prod", GROUPS)
         rprod = half_tiles("rprod", GROUPS)
-        rpair = half_tiles("rpair", GROUPS * 2)
+        rpair = [spare[1][:], rate[0][:, : GROUPS * 2]]
         rkept = half_tiles("rkept", HALF)
         k4 = [kept[:, cols[h]].rearrange("p (v a e) -> p v a e", a=2, e=2) for h in range(HALVES)]
         H = range(HALVES)
-        rate = half_tiles("rate", HALF)
         met = half_tiles("met", HALF)
         top = half_tiles("top", GROUPS)
         diff = half_tiles("diff", HALF)
@@ -106,7 +109,7 @@ def tile_picked_ypf_put_p_kernel(tc, x_words, x_scales, w1, avg, offs, usr, out)
             return t.unsqueeze(2).to_broadcast([P, GROUPS, D])
 
         def s_pair(h):
-            nc.vector.tensor_tensor(paired(pair[h][:]), k4[h][:, :, 0, :], k4[h][:, :, 1, :], ALU.mult)
+            nc.vector.tensor_tensor(paired(pair[h]), k4[h][:, :, 0, :], k4[h][:, :, 1, :], ALU.mult)
 
         def s_prod(h):
             nc.vector.tensor_tensor(prod[h][:], pair[h][:, 0::2], pair[h][:, 1::2], ALU.mult)
@@ -115,15 +118,15 @@ def tile_picked_ypf_put_p_kernel(tc, x_words, x_scales, w1, avg, offs, usr, out)
             nc.vector.reciprocal(rprod[h][:], prod[h][:])
 
         def s_rpair(h):
-            nc.vector.tensor_tensor(paired(rpair[h][:]), paired(pair[h][:])[:, :, ::-1],
+            nc.vector.tensor_tensor(paired(rpair[h]), paired(pair[h])[:, :, ::-1],
                                     rprod[h][:].unsqueeze(2).to_broadcast([P, GROUPS, 2]), ALU.mult)
 
         def s_rkept(h):
             nc.vector.tensor_tensor(rkept[h][:].rearrange("p (v a e) -> p v a e", a=2, e=2), k4[h][:, :, ::-1, :],
-                                    paired(rpair[h][:]).unsqueeze(2).to_broadcast([P, GROUPS, 2, 2]), ALU.mult)
+                                    paired(rpair[h]).unsqueeze(2).to_broadcast([P, GROUPS, 2, 2]), ALU.mult)
 
         def s_rate(h):
-            nc.vector.scalar_tensor_tensor(rate[h][:], lns[:, cols[h]], -1.0, y[h][:], ALU.mult, ALU.max)
+            nc.vector.scalar_tensor_tensor(rate[h][:], lns[h], -1.0, y[h][:], ALU.mult, ALU.max)
 
         def s_met(h):
             nc.vector.tensor_tensor(met[h][:], rate[h][:], rkept[h][:], ALU.mult)
@@ -147,31 +150,31 @@ def tile_picked_ypf_put_p_kernel(tc, x_words, x_scales, w1, avg, offs, usr, out)
         def s_gain(h):
             nc.vector.scalar_tensor_tensor(grouped(gain[:, cols[h]]), grouped(exrate[h][:]), 0.2, spread(rtotal[h][:]), ALU.mult, ALU.mult)
 
-        s_pair(0)
         s_pair(1)
-        s_prod(0)
+        s_pair(0)
         s_prod(1)
-        s_rprod(0)
+        s_prod(0)
         s_rprod(1)
-        s_rpair(0)
+        s_rprod(0)
         s_rpair(1)
-        s_rkept(0)
-        s_rate(0)
+        s_rpair(0)
         s_rkept(1)
-        s_met(0)
         s_rate(1)
-        s_top(0)
+        s_rkept(0)
         s_met(1)
-        s_ex(0)
+        s_rate(0)
         s_top(1)
+        s_met(0)
         s_ex(1)
-        s_total(0)
-        s_exrate(0)
-        s_rtotal(0)
+        s_top(0)
+        s_ex(0)
         s_total(1)
         s_exrate(1)
         s_rtotal(1)
-        s_gain(0)
+        s_total(0)
+        s_exrate(0)
+        s_rtotal(0)
         s_gain(1)
+        s_gain(0)
         nc.vector.tensor_tensor(window[:].indirect(usr_sb[:]), gain[:], kept[:], ALU.add)
         nc.sync.dma_start(out, window[:, :U])

@@ -39,15 +39,15 @@ def tile_picked_ypf_put_p_kernel(tc, x_words, x_scales, w1, avg, offs, usr, out)
         tiny = sb.tile([P, 1], F32, name="tiny")
 
         nc.vector.memset(xs[:].bitcast(I32), 0)
-        nc.gpsimd.memset(window[:, U:], 0.0)
-        nc.gpsimd.memset(tiny[:], TINY)
+        nc.vector.memset(window[:, U:], 0.0)
+        nc.vector.memset(tiny[:], TINY)
 
-        nc.sync.dma_start(offs_sb[:], offs)
         nc.sync.dma_start(w_raw[:], w1.rearrange("(p j) n -> p j n", j=4))
+        nc.sync.dma_start(offs_sb[:], offs)
+        nc.sync.dma_start(usr_sb[:], usr)
         for r in range(4):
             nc.sync.dma_start(xs[r:P:32, :].bitcast(I32), x_scales[0, r:16:4, :].bitcast(I32))
         nc.sync.dma_start(xw[:], x_words[0].rearrange("p c r -> p (c r)").bitcast(I32))
-        nc.sync.dma_start(usr_sb[:], usr)
         nc.sync.dma_start(window[:, :U], avg)
 
         w_bf = sb.tile([P, N, 4], BF16, name="w_bf", align_bytes=64)

@@ -15,11 +15,13 @@ AXIS_X = mybir.AxisListType.X
 
 P = 128
 K, T, S, D, N, U = 512, 2048, 512, 4, 128, 1024
-HALVES = 2
-HALF = S // HALVES
+PACK = 4
+LIST_ROWS = 16
+HALVES = range(2)
+HALF = S // 2
 GROUPS = HALF // D
-AVG_WINDOW = 2 * U
 TINY = 2.0 ** -60
+LN_OVERLAP = 8
 
 FLOPS = 2 * K * N * S
 
@@ -30,73 +32,84 @@ def tile_picked_ypf_put_p_kernel(tc, x_words, x_scales, w1, avg, offs, usr, out)
         sb = ctx.enter_context(tc.tile_pool(name="sb", bufs=1))
         ps = ctx.enter_context(tc.psum_pool(name="ps", bufs=1))
 
-        offs_sb = sb.tile([P, S // 16], U16, name="offs_sb")
-        usr_sb = sb.tile([P, S // 16], U16, name="usr_sb")
+        offs_sb = sb.tile([P, S // LIST_ROWS], U16, name="offs_sb")
+        usr_sb = sb.tile([P, S // LIST_ROWS], U16, name="usr_sb")
         xw = sb.tile([P, T], I32, name="xw", align_bytes=64)
         xs = sb.tile([P, T], U8, name="xs", align_bytes=64)
-        w_raw = sb.tile([P, 4, N], F32, name="w_raw")
-        window = sb.tile([P, AVG_WINDOW], F32, name="window", align_bytes=64)
+        w_raw = sb.tile([P, PACK, N], F32, name="w_raw")
+        window = sb.tile([P, U], F32, name="window", align_bytes=64)
         tiny = sb.tile([P, 1], F32, name="tiny")
 
         nc.vector.memset(xs[:].bitcast(I32), 0)
-        nc.vector.memset(window[:, U:], 0.0)
         nc.vector.memset(tiny[:], TINY)
 
-        nc.sync.dma_start(w_raw[:], w1.rearrange("(p j) n -> p j n", j=4))
+        nc.sync.dma_start(w_raw[:], w1.rearrange("(p j) n -> p j n", j=PACK))
         nc.sync.dma_start(offs_sb[:], offs)
         nc.sync.dma_start(usr_sb[:], usr)
         for r in range(4):
             nc.sync.dma_start(xs[r:P:32, :].bitcast(I32), x_scales[0, r:16:4, :].bitcast(I32))
         nc.sync.dma_start(xw[:], x_words[0].rearrange("p c r -> p (c r)").bitcast(I32))
-        nc.sync.dma_start(window[:, :U], avg)
+        nc.sync.dma_start(window[:], avg)
 
-        w_bf = sb.tile([P, N, 4], BF16, name="w_bf", align_bytes=64)
+        w_bf = sb.tile([P, N, PACK], BF16, name="w_bf", align_bytes=64)
         w_codes = sb.tile([P, N], U32, name="w_codes", align_bytes=64)
         w_scales = sb.tile([P, N], U8, name="w_scales", align_bytes=64)
         nc.scalar.copy(w_bf[:], w_raw[:].rearrange("p j n -> p n j"))
-        gs = sb.tile([P, S], U8, name="gs", align_bytes=64)
-        nc.vector.tensor_copy(gs[:], xs[:].indirect(offs_sb[:]))
-        nc.vector.quantize_mx(out=w_codes[:].bitcast(FP8X4), scales=w_scales[:], in_=w_bf[:].rearrange("p n j -> p (n j)"))
+        picked_scales = sb.tile([P, S], U8, name="picked_scales", align_bytes=64)
+        nc.vector.tensor_copy(picked_scales[:], xs[:].indirect(offs_sb[:]))
+        nc.vector.quantize_mx(
+            out=w_codes[:].bitcast(FP8X4), scales=w_scales[:], in_=w_bf[:].rearrange("p n j -> p (n j)")
+        )
 
-        cols = [slice(h * HALF, (h + 1) * HALF) for h in range(HALVES)]
-        lcols = [slice(h * HALF // 16, (h + 1) * HALF // 16) for h in range(HALVES)]
+        cols = [slice(h * HALF, (h + 1) * HALF) for h in HALVES]
+        list_cols = [slice(h * HALF // LIST_ROWS, (h + 1) * HALF // LIST_ROWS) for h in HALVES]
+
         sig = sb.tile([P, S], F32, name="sig")
         y = []
-        for h in range(HALVES):
-            gw = sb.tile([P, HALF], U32, name="gw%d" % h, align_bytes=64)
-            nc.vector.tensor_copy(gw[:], xw[:].bitcast(U32).indirect(offs_sb[:, lcols[h]]))
-            yh = ps.tile([P, HALF], F32, name="y%d" % h)
-            nc.tensor.matmul_mx(out=yh[:], lhsT=w_codes[:].bitcast(FP8X4), lhsT_scale=w_scales[:],
-                                rhs=gw[:].bitcast(FP8X4), rhs_scale=gs[:, cols[h]], start=True, stop=True)
-            nc.scalar.activation(sig[:, cols[h]], yh[:], ACT.Sigmoid, scale=-1.0)
-            y.append(yh)
-        ln_lead = sb.tile([P, HALF], F32, name="ln_lead")
-        lns = [sig[:, cols[1]], ln_lead[:]]
-        nc.scalar.activation(lns[1], sig[:, cols[1]], ACT.Ln, bias=tiny[:])
-        nc.scalar.activation(lns[0], sig[:, cols[0]], ACT.Ln, bias=tiny[:])
+        for h in HALVES:
+            picked_words = sb.tile([P, HALF], U32, name="picked_words%d" % h, align_bytes=64)
+            nc.vector.tensor_copy(picked_words[:], xw[:].bitcast(U32).indirect(offs_sb[:, list_cols[h]]))
+            y_half = ps.tile([P, HALF], F32, name="y%d" % h)
+            nc.tensor.matmul_mx(
+                out=y_half[:],
+                lhsT=w_codes[:].bitcast(FP8X4),
+                lhsT_scale=w_scales[:],
+                rhs=picked_words[:].bitcast(FP8X4),
+                rhs_scale=picked_scales[:, cols[h]],
+                start=True,
+                stop=True,
+            )
+            nc.scalar.activation(sig[:, cols[h]], y_half[:], ACT.Sigmoid, scale=-1.0)
+            y.append(y_half)
+
+        ln_all = sb.tile([P, S], F32, name="ln_all")
+        for part in (slice(0, HALF + LN_OVERLAP), slice(HALF + LN_OVERLAP, S)):
+            nc.scalar.activation(ln_all[:, part], sig[:, part], ACT.Ln, bias=tiny[:])
+        ln_sig = [ln_all[:, cols[h]] for h in HALVES]
 
         kept = sb.tile([P, S], F32, name="kept")
-        nc.vector.tensor_scalar(kept[:], window[:].indirect(usr_sb[:]), 0.8, 0.0, ALU.mult, ALU.add)
 
         def half_tiles(name, width):
-            return [sb.tile([P, width], F32, name="%s%d" % (name, h)) for h in range(HALVES)]
+            return [sb.tile([P, width], F32, name="%s%d" % (name, h)) for h in HALVES]
 
+        ag_all = sb.tile([P, S], F32, name="ag_all")
+        ag = [ag_all[:, cols[h]] for h in HALVES]
         rate = half_tiles("rate", HALF)
-        spare = half_tiles("spare", GROUPS * 2)
-        pair = [spare[0][:], rate[1][:, : GROUPS * 2]]
+        pair_second = sb.tile([P, GROUPS * 2], F32, name="pair_second")
+        inv_pair_second = sb.tile([P, GROUPS * 2], F32, name="inv_pair_second")
+        pair = [rate[0][:, : GROUPS * 2], pair_second[:]]
         prod = half_tiles("prod", GROUPS)
-        rprod = half_tiles("rprod", GROUPS)
-        rpair = [spare[1][:], rate[0][:, : GROUPS * 2]]
-        rkept = half_tiles("rkept", HALF)
-        k4 = [kept[:, cols[h]].rearrange("p (v a e) -> p v a e", a=2, e=2) for h in range(HALVES)]
-        H = range(HALVES)
+        inv_prod = half_tiles("inv_prod", GROUPS)
+        inv_pair = [rate[1][:, : GROUPS * 2], inv_pair_second[:]]
+        inv_ag_first = sb.tile([P, HALF], F32, name="inv_ag_first")
+        inv_ag = [inv_ag_first[:], ln_sig[0]]
         met = half_tiles("met", HALF)
         top = half_tiles("top", GROUPS)
-        diff = half_tiles("diff", HALF)
+        diff = [kept[:, cols[h]] for h in HALVES]
         ex = half_tiles("ex", HALF)
         total = half_tiles("total", GROUPS)
-        rtotal = half_tiles("rtotal", GROUPS)
-        exrate = half_tiles("exrate", HALF)
+        inv_total = half_tiles("inv_total", GROUPS)
+        ex_rate = half_tiles("ex_rate", HALF)
         gain = sb.tile([P, S], F32, name="gain")
 
         def grouped(t):
@@ -105,76 +118,70 @@ def tile_picked_ypf_put_p_kernel(tc, x_words, x_scales, w1, avg, offs, usr, out)
         def paired(t):
             return t.rearrange("p (v e) -> p v e", e=2)
 
+        def two_by_two(t):
+            return t.rearrange("p (v a e) -> p v a e", a=2, e=2)
+
         def spread(t):
             return t.unsqueeze(2).to_broadcast([P, GROUPS, D])
 
-        def s_pair(h):
-            nc.vector.tensor_tensor(paired(pair[h]), k4[h][:, :, 0, :], k4[h][:, :, 1, :], ALU.mult)
+        def invert_averages(h):
+            nc.vector.tensor_tensor(
+                two_by_two(inv_ag[h]),
+                two_by_two(ag[h])[:, :, ::-1, :],
+                paired(inv_pair[h]).unsqueeze(2).to_broadcast([P, GROUPS, 2, 2]),
+                ALU.mult,
+            )
 
-        def s_prod(h):
-            nc.vector.tensor_tensor(prod[h][:], pair[h][:, 0::2], pair[h][:, 1::2], ALU.mult)
+        def make_rate(h):
+            nc.vector.scalar_tensor_tensor(rate[h][:], ln_sig[h], -1.0, y[h][:], ALU.mult, ALU.max)
 
-        def s_rprod(h):
-            nc.vector.reciprocal(rprod[h][:], prod[h][:])
+        def make_met(h):
+            nc.vector.tensor_tensor(met[h][:], rate[h][:], inv_ag[h], ALU.mult)
 
-        def s_rpair(h):
-            nc.vector.tensor_tensor(paired(rpair[h]), paired(pair[h])[:, :, ::-1],
-                                    rprod[h][:].unsqueeze(2).to_broadcast([P, GROUPS, 2]), ALU.mult)
-
-        def s_rkept(h):
-            nc.vector.tensor_tensor(rkept[h][:].rearrange("p (v a e) -> p v a e", a=2, e=2), k4[h][:, :, ::-1, :],
-                                    paired(rpair[h]).unsqueeze(2).to_broadcast([P, GROUPS, 2, 2]), ALU.mult)
-
-        def s_rate(h):
-            nc.vector.scalar_tensor_tensor(rate[h][:], lns[h], -1.0, y[h][:], ALU.mult, ALU.max)
-
-        def s_met(h):
-            nc.vector.tensor_tensor(met[h][:], rate[h][:], rkept[h][:], ALU.mult)
-
-        def s_top(h):
+        def make_top(h):
             nc.vector.tensor_reduce(top[h][:], grouped(met[h][:]), AXIS_X, ALU.max)
 
-        def s_ex(h):
-            nc.vector.tensor_tensor(grouped(diff[h][:]), grouped(met[h][:]), spread(top[h][:]), ALU.subtract)
-            nc.scalar.activation(ex[h][:], diff[h][:], ACT.Exp, scale=3.0 * 0.8)
+        def make_ex(h):
+            nc.vector.tensor_tensor(grouped(diff[h]), grouped(met[h][:]), spread(top[h][:]), ALU.subtract)
+            nc.scalar.activation(ex[h][:], diff[h], ACT.Exp, scale=3.0)
 
-        def s_total(h):
+        def make_total(h):
             nc.vector.tensor_reduce(total[h][:], grouped(ex[h][:]), AXIS_X, ALU.add)
 
-        def s_exrate(h):
-            nc.vector.tensor_tensor(exrate[h][:], ex[h][:], rate[h][:], ALU.mult)
+        def weigh_and_invert_total(h):
+            nc.vector.tensor_tensor(ex_rate[h][:], ex[h][:], rate[h][:], ALU.mult)
+            nc.vector.reciprocal(inv_total[h][:], total[h][:])
 
-        def s_rtotal(h):
-            nc.vector.reciprocal(rtotal[h][:], total[h][:])
+        for h in HALVES:
+            nc.vector.tensor_copy(ag[h], window[:].indirect(usr_sb[:, list_cols[h]]))
+        for h in HALVES:
+            nc.vector.tensor_tensor(paired(pair[h]), two_by_two(ag[h])[:, :, 0, :], two_by_two(ag[h])[:, :, 1, :], ALU.mult)
+        for h in HALVES:
+            nc.vector.tensor_tensor(prod[h][:], pair[h][:, 0::2], pair[h][:, 1::2], ALU.mult)
+        for h in HALVES:
+            nc.vector.reciprocal(inv_prod[h][:], prod[h][:])
+        for h in HALVES:
+            nc.vector.tensor_tensor(
+                paired(inv_pair[h]),
+                paired(pair[h])[:, :, ::-1],
+                inv_prod[h][:].unsqueeze(2).to_broadcast([P, GROUPS, 2]),
+                ALU.mult,
+            )
 
-        def s_gain(h):
-            nc.vector.scalar_tensor_tensor(grouped(gain[:, cols[h]]), grouped(exrate[h][:]), 0.2, spread(rtotal[h][:]), ALU.mult, ALU.mult)
+        invert_averages(0)
+        make_rate(0)
+        make_rate(1)
+        for lead, trail in ((make_met, invert_averages), (make_top, make_met), (make_ex, make_top), (make_total, make_ex)):
+            lead(0)
+            trail(1)
+        nc.scalar.activation(kept[:], ag_all[:], ACT.Copy, scale=0.8)
+        weigh_and_invert_total(0)
+        make_total(1)
+        weigh_and_invert_total(1)
+        for h in HALVES:
+            nc.vector.scalar_tensor_tensor(
+                grouped(gain[:, cols[h]]), grouped(ex_rate[h][:]), 0.2, spread(inv_total[h][:]), ALU.mult, ALU.mult
+            )
 
-        s_pair(1)
-        s_pair(0)
-        s_prod(1)
-        s_prod(0)
-        s_rprod(1)
-        s_rprod(0)
-        s_rpair(1)
-        s_rpair(0)
-        s_rkept(1)
-        s_rate(1)
-        s_rkept(0)
-        s_met(1)
-        s_rate(0)
-        s_top(1)
-        s_met(0)
-        s_ex(1)
-        s_top(0)
-        s_ex(0)
-        s_total(1)
-        s_exrate(1)
-        s_rtotal(1)
-        s_total(0)
-        s_exrate(0)
-        s_rtotal(0)
-        s_gain(1)
-        s_gain(0)
         nc.vector.tensor_tensor(window[:].indirect(usr_sb[:]), gain[:], kept[:], ALU.add)
-        nc.sync.dma_start(out, window[:, :U])
+        nc.sync.dma_start(out, window[:])

from contextlib import ExitStack

import concourse.mybir as mybir

F32 = mybir.dt.float32
BF16 = mybir.dt.bfloat16
I32 = mybir.dt.int32
U32 = mybir.dt.uint32
U16 = mybir.dt.uint16
U8 = mybir.dt.uint8
FP8X4 = mybir.dt.float8_e4m3fn_x4
ALU = mybir.AluOpType
ACT = mybir.ActivationFunctionType
AXIS_X = mybir.AxisListType.X

P = 128
K, T, S, D, N, U = 512, 2048, 512, 4, 128, 1024
PACK = 4
LIST_ROWS = 16
HALVES = range(2)
HALF = S // 2
GROUPS = HALF // D
TINY = 2.0 ** -60
LN_OVERLAP = 8

FLOPS = 2 * K * N * S


def tile_picked_ypf_put_p_kernel(tc, x_words, x_scales, w1, avg, offs, usr, out):
    nc = tc.nc
    with ExitStack() as ctx:
        sb = ctx.enter_context(tc.tile_pool(name="sb", bufs=1))
        ps = ctx.enter_context(tc.psum_pool(name="ps", bufs=1))

        offs_sb = sb.tile([P, S // LIST_ROWS], U16, name="offs_sb")
        usr_sb = sb.tile([P, S // LIST_ROWS], U16, name="usr_sb")
        xw = sb.tile([P, T], I32, name="xw", align_bytes=64)
        xs = sb.tile([P, T], U8, name="xs", align_bytes=64)
        w_raw = sb.tile([P, PACK, N], F32, name="w_raw")
        window = sb.tile([P, U], F32, name="window", align_bytes=64)
        tiny = sb.tile([P, 1], F32, name="tiny")

        nc.vector.memset(xs[:].bitcast(I32), 0)
        nc.vector.memset(tiny[:], TINY)

        nc.sync.dma_start(w_raw[:], w1.rearrange("(p j) n -> p j n", j=PACK))
        nc.sync.dma_start(offs_sb[:], offs)
        nc.sync.dma_start(usr_sb[:], usr)
        for r in range(4):
            nc.sync.dma_start(xs[r:P:32, :].bitcast(I32), x_scales[0, r:16:4, :].bitcast(I32))
        nc.sync.dma_start(xw[:], x_words[0].rearrange("p c r -> p (c r)").bitcast(I32))
        nc.sync.dma_start(window[:], avg)

        w_bf = sb.tile([P, N, PACK], BF16, name="w_bf", align_bytes=64)
        w_codes = sb.tile([P, N], U32, name="w_codes", align_bytes=64)
        w_scales = sb.tile([P, N], U8, name="w_scales", align_bytes=64)
        nc.scalar.copy(w_bf[:], w_raw[:].rearrange("p j n -> p n j"))
        picked_scales = sb.tile([P, S], U8, name="picked_scales", align_bytes=64)
        nc.vector.tensor_copy(picked_scales[:], xs[:].indirect(offs_sb[:]))
        nc.vector.quantize_mx(
            out=w_codes[:].bitcast(FP8X4), scales=w_scales[:], in_=w_bf[:].rearrange("p n j -> p (n j)")
        )

        cols = [slice(h * HALF, (h + 1) * HALF) for h in HALVES]
        list_cols = [slice(h * HALF // LIST_ROWS, (h + 1) * HALF // LIST_ROWS) for h in HALVES]

        sig = sb.tile([P, S], F32, name="sig")
        y = []
        for h in HALVES:
            picked_words = sb.tile([P, HALF], U32, name="picked_words%d" % h, align_bytes=64)
            nc.vector.tensor_copy(picked_words[:], xw[:].bitcast(U32).indirect(offs_sb[:, list_cols[h]]))
            y_half = ps.tile([P, HALF], F32, name="y%d" % h)
            nc.tensor.matmul_mx(
                out=y_half[:],
                lhsT=w_codes[:].bitcast(FP8X4),
                lhsT_scale=w_scales[:],
                rhs=picked_words[:].bitcast(FP8X4),
                rhs_scale=picked_scales[:, cols[h]],
                start=True,
                stop=True,
            )
            nc.scalar.activation(sig[:, cols[h]], y_half[:], ACT.Sigmoid, scale=-1.0)
            y.append(y_half)

        ln_all = sb.tile([P, S], F32, name="ln_all")
        for part in (slice(0, HALF + LN_OVERLAP), slice(HALF + LN_OVERLAP, S)):
            nc.scalar.activation(ln_all[:, part], sig[:, part], ACT.Ln, bias=tiny[:])
        ln_sig = [ln_all[:, cols[h]] for h in HALVES]

        kept = sb.tile([P, S], F32, name="kept")

        def half_tiles(name, width):
            return [sb.tile([P, width], F32, name="%s%d" % (name, h)) for h in HALVES]

        ag_all = sb.tile([P, S], F32, name="ag_all")
        ag = [ag_all[:, cols[h]] for h in HALVES]
        rate = half_tiles("rate", HALF)
        pair_second = sb.tile([P, GROUPS * 2], F32, name="pair_second")
        inv_pair_second = sb.tile([P, GROUPS * 2], F32, name="inv_pair_second")
        pair = [rate[0][:, : GROUPS * 2], pair_second[:]]
        prod = half_tiles("prod", GROUPS)
        inv_prod = half_tiles("inv_prod", GROUPS)
        inv_pair = [rate[1][:, : GROUPS * 2], inv_pair_second[:]]
        inv_ag_first = sb.tile([P, HALF], F32, name="inv_ag_first")
        inv_ag = [inv_ag_first[:], ln_sig[0]]
        met = half_tiles("met", HALF)
        top = half_tiles("top", GROUPS)
        diff = [kept[:, cols[h]] for h in HALVES]
        ex = half_tiles("ex", HALF)
        total = half_tiles("total", GROUPS)
        inv_total = half_tiles("inv_total", GROUPS)
        ex_rate = half_tiles("ex_rate", HALF)
        gain = sb.tile([P, S], F32, name="gain")

        def grouped(t):
            return t.rearrange("p (v d) -> p v d", d=D)

        def paired(t):
            return t.rearrange("p (v e) -> p v e", e=2)

        def two_by_two(t):
            return t.rearrange("p (v a e) -> p v a e", a=2, e=2)

        def spread(t):
            return t.unsqueeze(2).to_broadcast([P, GROUPS, D])

        def invert_averages(h):
            nc.vector.tensor_tensor(
                two_by_two(inv_ag[h]),
                two_by_two(ag[h])[:, :, ::-1, :],
                paired(inv_pair[h]).unsqueeze(2).to_broadcast([P, GROUPS, 2, 2]),
                ALU.mult,
            )

        def make_rate(h):
            nc.vector.scalar_tensor_tensor(rate[h][:], ln_sig[h], -1.0, y[h][:], ALU.mult, ALU.max)

        def make_met(h):
            nc.vector.tensor_tensor(met[h][:], rate[h][:], inv_ag[h], ALU.mult)

        def make_top(h):
            nc.vector.tensor_reduce(top[h][:], grouped(met[h][:]), AXIS_X, ALU.max)

        def make_ex(h):
            nc.vector.tensor_tensor(grouped(diff[h]), grouped(met[h][:]), spread(top[h][:]), ALU.subtract)
            nc.scalar.activation(ex[h][:], diff[h], ACT.Exp, scale=3.0)

        def make_total(h):
            nc.vector.tensor_reduce(total[h][:], grouped(ex[h][:]), AXIS_X, ALU.add)

        def weigh_and_invert_total(h):
            nc.vector.tensor_tensor(ex_rate[h][:], ex[h][:], rate[h][:], ALU.mult)
            nc.vector.reciprocal(inv_total[h][:], total[h][:])

        for h in HALVES:
            nc.vector.tensor_copy(ag[h], window[:].indirect(usr_sb[:, list_cols[h]]))
        for h in HALVES:
            nc.vector.tensor_tensor(paired(pair[h]), two_by_two(ag[h])[:, :, 0, :], two_by_two(ag[h])[:, :, 1, :], ALU.mult)
        for h in HALVES:
            nc.vector.tensor_tensor(prod[h][:], pair[h][:, 0::2], pair[h][:, 1::2], ALU.mult)
        for h in HALVES:
            nc.vector.reciprocal(inv_prod[h][:], prod[h][:])
        for h in HALVES:
            nc.vector.tensor_tensor(
                paired(inv_pair[h]),
                paired(pair[h])[:, :, ::-1],
                inv_prod[h][:].unsqueeze(2).to_broadcast([P, GROUPS, 2]),
                ALU.mult,
            )

        invert_averages(0)
        make_rate(0)
        make_rate(1)
        for lead, trail in ((make_met, invert_averages), (make_top, make_met), (make_ex, make_top), (make_total, make_ex)):
            lead(0)
            trail(1)
        nc.scalar.activation(kept[:], ag_all[:], ACT.Copy, scale=0.8)
        weigh_and_invert_total(0)
        make_total(1)
        weigh_and_invert_total(1)
        for h in HALVES:
            nc.vector.scalar_tensor_tensor(
                grouped(gain[:, cols[h]]), grouped(ex_rate[h][:]), 0.2, spread(inv_total[h][:]), ALU.mult, ALU.mult
            )

        nc.vector.tensor_tensor(window[:].indirect(usr_sb[:]), gain[:], kept[:], ALU.add)
        nc.sync.dma_start(out, window[:])
